import numpy as np
import ml_dtypes


def mxq(x, axis, fmt="e4m3"):
    dtype, down = {"e4m3": (ml_dtypes.float8_e4m3fn, 7), "e5m2": (ml_dtypes.float8_e5m2, 14)}[fmt]
    v = np.moveaxis(np.asarray(x, np.float32).astype(ml_dtypes.bfloat16).astype(np.float64), axis, -1)
    blocks = v.reshape(v.shape[:-1] + (-1, 32))
    amax = np.abs(blocks).max(-1, keepdims=True)
    byte = np.maximum(np.where(amax > 0, np.frexp(amax)[1] - 1 + 127, 0) - down, 1)
    scale = np.exp2(byte - 127.0)
    codes = (blocks / scale).astype(np.float32).astype(dtype).astype(np.float64)
    return np.moveaxis((codes * scale).reshape(v.shape), -1, axis)


WIDE = False


def mx_kscale(k):
    if not WIDE:
        return np.ones(k)
    levels = np.array([10, -10, 5, -5, 0])
    if k % 512:
        return np.exp2(np.random.permutation(np.resize(levels, k // 32))).repeat(32)
    a = np.empty((k // 512, 16))
    for p in range(k // 512):
        a[p, :8] = np.random.permutation(np.resize(levels, 8))
        for g in range(8):
            far = levels[np.abs(levels - a[p, g]) >= 10]
            a[p, g + 8] = far[np.random.randint(len(far))]
    return np.exp2(a.ravel()).repeat(32)


def f64(x):
    return np.asarray(x).astype(np.float64)


def striped(idx):
    return np.tile(idx.reshape(-1, 16).T, (8, 1)).astype(np.uint16)


def unstriped(offs):
    return offs[:16].T.reshape(-1).astype(np.int64)


E2M1 = np.array([0.0, 0.5, 1.0, 1.5, 2.0, 3.0, 4.0, 6.0, -0.0, -0.5, -1.0, -1.5, -2.0, -3.0, -4.0, -6.0])


def pack_weight(w, fmt):
    k, n = w.shape
    w = f64(np.asarray(w, np.float32).astype(ml_dtypes.bfloat16)).reshape(k // 32, 32, n)
    amax = np.abs(w).max(1)
    if fmt == "e4m3":
        byte = np.frexp(amax)[1] - 1 + 127 - 7
    else:
        mant, ex = np.frexp(amax / 6.0)
        byte = np.where(mant > 0.5, ex, ex - 1) + 127
    byte = np.clip(np.where(amax > 0, byte, 1), 1, 254)
    scaled = (w * np.exp2(127.0 - byte)[:, None, :]).reshape(k, n).astype(np.float32)
    by_word = np.ascontiguousarray(scaled.reshape(k // 512, 128, 4, n).transpose(0, 1, 3, 2))
    if fmt == "e4m3":
        words = by_word.astype(ml_dtypes.float8_e4m3fn).view(np.uint8)
    else:
        c = by_word.astype(ml_dtypes.float4_e2m1fn).view(np.uint8) & 0xF
        words = (c[..., 0::2] | (c[..., 1::2] << 4)).reshape(k // 512, 128, 2 * n)
    return np.ascontiguousarray(words), np.ascontiguousarray(byte.astype(np.uint8).reshape(k // 512, 16, n))


def unpack_weight(words, scales, fmt):
    g, _, n = scales.shape
    words = np.ascontiguousarray(words).reshape(g, 128, n, -1)
    if fmt == "e4m3":
        vals = words.view(ml_dtypes.float8_e4m3fn).astype(np.float64)
    else:
        nib = np.empty((g, 128, n, 4), np.uint8)
        nib[..., 0::2] = words & 0xF
        nib[..., 1::2] = words >> 4
        vals = E2M1[nib]
    vals = vals * np.repeat(np.exp2(scales.astype(np.float64) - 127.0), 8, axis=1)[..., None]
    return vals.transpose(0, 1, 3, 2).reshape(g * 512, n)


def pack_table(v):
    words, scales = pack_weight(v, "e4m3")
    return np.concatenate([words.reshape(words.shape[0], -1), scales.reshape(scales.shape[0], -1)], axis=1)


def unpack_table(tab):
    g, t = tab.shape[0], tab.shape[1] // 528
    return unpack_weight(tab[:, :512 * t].reshape(g, 128, t, 4), tab[:, 512 * t:].reshape(g, 16, t), "e4m3")


def silu(v):
    return v / (1.0 + np.exp(-np.maximum(v, -700.0)))


K, M, T, S = 1024, 256, 4096, 2048


def setup_inputs():
    n = np.random.standard_normal
    s = mx_kscale(K)[:, None]
    return {
        "tab": pack_table(n((K, T)) * s),
        "w": (n((K, M)) / np.sqrt(K) / s).astype(np.float32),
        "b": (0.3 * n(256)).astype(np.float32),
        "wgo": np.tile(np.random.uniform(0.5, 2.0, S), (128, 1)).astype(np.float32),
        "offs": striped(np.random.permutation(T)[:S]),
        "offs2": striped(np.random.permutation(T)[:S]),
    }


def reference(tab, w, b, wgo, offs, offs2):
    tab_ = unpack_table(tab)[:, unstriped(offs)]
    w_ = mxq(f64(w), 0, "e4m3")
    y = w_.T @ tab_
    out = np.zeros((M, T))
    out[:, unstriped(offs2)] = f64(wgo)[0] * (silu(y + f64(b)[:, None]))
    return out

@@ -1,0 +1,124 @@
+import concourse.mybir as mybir
+
+K, M, T, S = 1024, 256, 4096, 2048
+P = 128
+PASSES = K // 512
+M_TILES = M // P
+N_TILE = 512
+SLICES = S // N_TILE
+COLS = N_TILE // 16
+
+F32 = mybir.dt.float32
+BF16 = mybir.dt.bfloat16
+I32 = mybir.dt.int32
+U32 = mybir.dt.uint32
+U16 = mybir.dt.uint16
+U8 = mybir.dt.uint8
+FP8X4 = mybir.dt.float8_e4m3fn_x4
+MULT = mybir.AluOpType.mult
+SILU = mybir.ActivationFunctionType.Silu
+
+FLOPS = 2 * K * M * S
+
+
+def tile_list_tabscat_silu_kernel(tc, tab, w, b, wgo, offs, offs2, out):
+    nc = tc.nc
+    with tc.tile_pool(name="hold", bufs=1) as hold, tc.psum_pool(name="psum", bufs=1) as psum:
+        list_in = hold.tile([P, S // 16], U16, name="list_in")
+        list_out = hold.tile([P, S // 16], U16, name="list_out")
+        nc.sync.dma_start(list_in[:], offs)
+
+        warm = hold.tile([P, 1], F32, name="warm")
+        nc.gpsimd.memset(warm[:], 0.0)
+        warmed = hold.tile([P, 1], F32, name="warmed")
+        nc.scalar.activation(warmed[:], warm[:], SILU)
+
+        scales = hold.tile([P, T], U8, name="scales", align_bytes=64)
+        nc.vector.memset(scales[:].bitcast(I32), 0)
+        for a in range(PASSES):
+            rows = tab[a, 512 * T : 528 * T].rearrange("(q t) -> q t", q=16)
+            queue = nc.sync if a == 0 else nc.scalar
+            for quad in range(4):
+                p0 = 32 * quad + 4 * a
+                queue.dma_start(scales[p0 : p0 + 4, :].bitcast(I32), rows[4 * quad : 4 * quad + 4, :].bitcast(I32))
+
+        words = [hold.tile([P, T], I32, name=f"words{a}", align_bytes=64) for a in range(PASSES)]
+        for a in range(PASSES):
+            nc.sync.dma_start(words[a][:], tab[a, 0 : 512 * T].rearrange("(p x) -> p x", p=P).bitcast(I32))
+
+        w_raw = [hold.tile([P, 4, M], F32, name=f"w_raw{a}") for a in range(PASSES)]
+        for a in range(PASSES):
+            nc.sync.dma_start(w_raw[a][:], w[512 * a : 512 * (a + 1), :].rearrange("(p j) n -> p j n", j=4))
+        bias = hold.tile([P, M_TILES], F32, name="bias")
+        nc.sync.dma_start(bias[:], b.rearrange("(m p) -> p m", p=P))
+        weight_out = hold.tile([P, S], F32, name="weight_out")
+        nc.sync.dma_start(weight_out[:], wgo)
+        nc.sync.dma_start(list_out[:], offs2)
+
+        windows = [hold.tile([P, T], F32, name=f"window{m}") for m in range(M_TILES)]
+        nc.vector.memset(windows[0][:], 0.0)
+        nc.gpsimd.memset(windows[1][:], 0.0)
+
+        picked_scales = hold.tile([P, S], U8, name="picked_scales", align_bytes=64)
+        nc.vector.tensor_copy(picked_scales[:], scales[:].indirect(list_in[:]))
+        picked = [hold.tile([P, S], U32, name=f"picked{a}", align_bytes=64) for a in range(PASSES)]
+        nc.vector.tensor_copy(picked[0][:], words[0][:].bitcast(U32).indirect(list_in[:]))
+
+        w_inter = hold.tile([P, M_TILES, PASSES, P, 4], BF16, name="w_inter", align_bytes=64)
+        w_codes = hold.tile([P, M_TILES, PASSES, P], U32, name="w_codes", align_bytes=64)
+        w_scales = hold.tile([P, M_TILES, PASSES, P], U8, name="w_scales", align_bytes=64)
+        for a in range(PASSES):
+            for m in range(M_TILES):
+                nc.scalar.copy(w_inter[:, m, a, :, :], w_raw[a][:, :, P * m : P * (m + 1)].rearrange("p j n -> p n j"))
+
+        def quantise(m):
+            nc.vector.quantize_mx(
+                out=w_codes[:, m, :, :].rearrange("p a n -> p (a n)").bitcast(FP8X4),
+                scales=w_scales[:, m, :, :].rearrange("p a n -> p (a n)"),
+                in_=w_inter[:, m, :, :, :].rearrange("p a n j -> p (a n j)"),
+            )
+
+        def gather_last(s):
+            cols = slice(N_TILE * s, N_TILE * (s + 1))
+            nc.vector.tensor_copy(picked[1][:, cols], words[1][:].bitcast(U32).indirect(list_in[:, COLS * s : COLS * (s + 1)]))
+
+        results = [hold.tile([P, S], F32, name=f"result{m}") for m in range(M_TILES)]
+
+        def multiply(m, s):
+            cols = slice(N_TILE * s, N_TILE * (s + 1))
+            acc = psum.tile([P, N_TILE], F32, name=f"acc{m}_{s}")
+            for a in range(PASSES):
+                nc.tensor.matmul_mx(
+                    out=acc[:],
+                    lhsT=w_codes[:, m, a, :].bitcast(FP8X4),
+                    lhsT_scale=w_scales[:, m, a, :],
+                    rhs=picked[a][:, cols].bitcast(FP8X4),
+                    rhs_scale=picked_scales[4 * a : P, cols],
+                    start=(a == 0),
+                    stop=(a == PASSES - 1),
+                )
+            nc.scalar.activation(results[m][:, cols], acc[:], SILU, bias=bias[:, m : m + 1])
+
+        def scatter(m, first, last):
+            cols = slice(N_TILE * first, N_TILE * last)
+            nc.vector.tensor_tensor(
+                windows[m][:].indirect(list_out[:, COLS * first : COLS * last]),
+                results[m][:, cols],
+                weight_out[:, cols],
+                MULT,
+            )
+
+        gather_last(0)
+        gather_last(1)
+        gather_last(2)
+        quantise(0)
+        gather_last(3)
+        quantise(1)
+        for m in range(M_TILES):
+            for s in range(SLICES):
+                multiply(m, s)
+        scatter(0, 0, 1)
+        scatter(0, 1, SLICES)
+        nc.sync.dma_start(out[0:P, :], windows[0][:])
+        scatter(1, 0, SLICES)
+        nc.sync.dma_start(out[P : 2 * P, :], windows[1][:])

@@ -28,30 +28,34 @@ def tile_list_tabscat_silu_kernel(tc, tab, w, b, wgo, offs, offs2, out):
         list_out = hold.tile([P, S // 16], U16, name="list_out")
         nc.sync.dma_start(list_in[:], offs)
 
-        warm = hold.tile([P, 1], F32, name="warm")
-        nc.gpsimd.memset(warm[:], 0.0)
-        warmed = hold.tile([P, 1], F32, name="warmed")
-        nc.scalar.activation(warmed[:], warm[:], SILU)
-
         scales = hold.tile([P, T], U8, name="scales", align_bytes=64)
-        nc.vector.memset(scales[:].bitcast(I32), 0)
-        for a in range(PASSES):
-            rows = tab[a, 512 * T : 528 * T].rearrange("(q t) -> q t", q=16)
-            queue = nc.sync if a == 0 else nc.scalar
-            for quad in range(4):
-                p0 = 32 * quad + 4 * a
-                queue.dma_start(scales[p0 : p0 + 4, :].bitcast(I32), rows[4 * quad : 4 * quad + 4, :].bitcast(I32))
+        scale_words = scales[:].bitcast(I32)
+        nc.gpsimd.memset(scale_words[:, 0 : 3 * T // 16], 0)
+        nc.vector.memset(scale_words[:, 3 * T // 16 : T // 4], 0)
+        scale_rows = tab[:, 512 * T : 528 * T].rearrange("a (q t) -> a q t", q=16)
+        for quad in range(4):
+            rows = scale_rows[:, 4 * quad : 4 * quad + 4, :].bitcast(I32)
+            if quad < 2:
+                for a in range(PASSES):
+                    p0 = 32 * quad + 4 * a
+                    nc.sync.dma_start(scale_words[p0 : p0 + 4, :], rows[a])
+            else:
+                nc.sync.dma_start(scale_words[32 * quad : 32 * quad + 8, :], rows)
 
         words = [hold.tile([P, T], I32, name=f"words{a}", align_bytes=64) for a in range(PASSES)]
-        for a in range(PASSES):
-            nc.sync.dma_start(words[a][:], tab[a, 0 : 512 * T].rearrange("(p x) -> p x", p=P).bitcast(I32))
-
         w_raw = [hold.tile([P, 4, M], F32, name=f"w_raw{a}") for a in range(PASSES)]
+        word_rows = [tab[a, 0 : 512 * T].rearrange("(p x) -> p x", p=P).bitcast(I32) for a in range(PASSES)]
+        weight_out = hold.tile([P, S], F32, name="weight_out")
+        for tile in (words[0][:, 0:8], words[1][:, 0:8]):
+            nc.gpsimd.memset(tile, 0)
+        for tile in (w_raw[0][:, 0, 0:8], w_raw[1][:, 0, 0:8], weight_out[:, 0:8]):
+            nc.gpsimd.memset(tile, 0.0)
+        for a in range(PASSES):
+            nc.sync.dma_start(words[a][:], word_rows[a])
         for a in range(PASSES):
             nc.sync.dma_start(w_raw[a][:], w[512 * a : 512 * (a + 1), :].rearrange("(p j) n -> p j n", j=4))
         bias = hold.tile([P, M_TILES], F32, name="bias")
         nc.sync.dma_start(bias[:], b.rearrange("(m p) -> p m", p=P))
-        weight_out = hold.tile([P, S], F32, name="weight_out")
         nc.sync.dma_start(weight_out[:], wgo)
         nc.sync.dma_start(list_out[:], offs2)
 
@@ -59,40 +63,52 @@ def tile_list_tabscat_silu_kernel(tc, tab, w, b, wgo, offs, offs2, out):
         nc.vector.memset(windows[0][:], 0.0)
         nc.gpsimd.memset(windows[1][:], 0.0)
 
+        warm = hold.tile([P, 1], F32, name="warm")
+        nc.vector.memset(warm[:], 0.0)
+        warmed = hold.tile([P, 1], F32, name="warmed")
+        nc.scalar.activation(warmed[:], warm[:], SILU)
+
         picked_scales = hold.tile([P, S], U8, name="picked_scales", align_bytes=64)
         nc.vector.tensor_copy(picked_scales[:], scales[:].indirect(list_in[:]))
-        picked = [hold.tile([P, S], U32, name=f"picked{a}", align_bytes=64) for a in range(PASSES)]
-        nc.vector.tensor_copy(picked[0][:], words[0][:].bitcast(U32).indirect(list_in[:]))
+        picked_first = hold.tile([P, S], U32, name="picked_first", align_bytes=64)
+        nc.vector.tensor_copy(picked_first[:], words[0][:].bitcast(U32).indirect(list_in[:]))
 
-        w_inter = hold.tile([P, M_TILES, PASSES, P, 4], BF16, name="w_inter", align_bytes=64)
+        w_inter = [
+            hold.tile([P, PASSES, P, 4], BF16, name=f"w_inter{m}", tag=f"turn{m}", align_bytes=64) for m in range(M_TILES)
+        ]
         w_codes = hold.tile([P, M_TILES, PASSES, P], U32, name="w_codes", align_bytes=64)
         w_scales = hold.tile([P, M_TILES, PASSES, P], U8, name="w_scales", align_bytes=64)
         for a in range(PASSES):
             for m in range(M_TILES):
-                nc.scalar.copy(w_inter[:, m, a, :, :], w_raw[a][:, :, P * m : P * (m + 1)].rearrange("p j n -> p n j"))
+                nc.scalar.copy(w_inter[m][:, a, :, :], w_raw[a][:, :, P * m : P * (m + 1)].rearrange("p j n -> p n j"))
 
         def quantise(m):
             nc.vector.quantize_mx(
                 out=w_codes[:, m, :, :].rearrange("p a n -> p (a n)").bitcast(FP8X4),
                 scales=w_scales[:, m, :, :].rearrange("p a n -> p (a n)"),
-                in_=w_inter[:, m, :, :, :].rearrange("p a n j -> p (a n j)"),
+                in_=w_inter[m][:].rearrange("p a n j -> p (a n j)"),
             )
 
-        def gather_last(s):
-            cols = slice(N_TILE * s, N_TILE * (s + 1))
-            nc.vector.tensor_copy(picked[1][:, cols], words[1][:].bitcast(U32).indirect(list_in[:, COLS * s : COLS * (s + 1)]))
+        def gather_half(h):
+            half = hold.tile([P, S // 2], U32, name=f"picked_last{h}", tag="turn0" if h else "picked_last0", align_bytes=64)
+            cols = slice(S // 32 * h, S // 32 * (h + 1))
+            nc.vector.tensor_copy(half[:], words[1][:].bitcast(U32).indirect(list_in[:, cols]))
+            return half
+
 
         results = [hold.tile([P, S], F32, name=f"result{m}") for m in range(M_TILES)]
 
         def multiply(m, s):
             cols = slice(N_TILE * s, N_TILE * (s + 1))
+            inner = slice(N_TILE * (s % 2), N_TILE * (s % 2 + 1))
+            rhs = [picked_first[:, cols], picked_last[s // 2][:, inner]]
             acc = psum.tile([P, N_TILE], F32, name=f"acc{m}_{s}")
             for a in range(PASSES):
                 nc.tensor.matmul_mx(
                     out=acc[:],
                     lhsT=w_codes[:, m, a, :].bitcast(FP8X4),
                     lhsT_scale=w_scales[:, m, a, :],
-                    rhs=picked[a][:, cols].bitcast(FP8X4),
+                    rhs=rhs[a].bitcast(FP8X4),
                     rhs_scale=picked_scales[4 * a : P, cols],
                     start=(a == 0),
                     stop=(a == PASSES - 1),
@@ -108,11 +124,9 @@ def tile_list_tabscat_silu_kernel(tc, tab, w, b, wgo, offs, offs2, out):
                 MULT,
             )
 
-        gather_last(0)
-        gather_last(1)
-        gather_last(2)
+        picked_last = [gather_half(0)]
         quantise(0)
-        gather_last(3)
+        picked_last.append(gather_half(1))
         quantise(1)
         for m in range(M_TILES):
             for s in range(SLICES):

@@ -30,12 +30,11 @@ def tile_list_tabscat_silu_kernel(tc, tab, w, b, wgo, offs, offs2, out):
 
         scales = hold.tile([P, T], U8, name="scales", align_bytes=64)
         scale_words = scales[:].bitcast(I32)
-        nc.gpsimd.memset(scale_words[:, 0 : 3 * T // 16], 0)
-        nc.vector.memset(scale_words[:, 3 * T // 16 : T // 4], 0)
+        nc.vector.memset(scale_words, 0)
         scale_rows = tab[:, 512 * T : 528 * T].rearrange("a (q t) -> a q t", q=16)
         for quad in range(4):
             rows = scale_rows[:, 4 * quad : 4 * quad + 4, :].bitcast(I32)
-            if quad < 2:
+            if quad < 3:
                 for a in range(PASSES):
                     p0 = 32 * quad + 4 * a
                     nc.sync.dma_start(scale_words[p0 : p0 + 4, :], rows[a])
@@ -47,9 +46,9 @@ def tile_list_tabscat_silu_kernel(tc, tab, w, b, wgo, offs, offs2, out):
         word_rows = [tab[a, 0 : 512 * T].rearrange("(p x) -> p x", p=P).bitcast(I32) for a in range(PASSES)]
         weight_out = hold.tile([P, S], F32, name="weight_out")
         for tile in (words[0][:, 0:8], words[1][:, 0:8]):
-            nc.gpsimd.memset(tile, 0)
+            nc.vector.memset(tile, 0)
         for tile in (w_raw[0][:, 0, 0:8], w_raw[1][:, 0, 0:8], weight_out[:, 0:8]):
-            nc.gpsimd.memset(tile, 0.0)
+            nc.vector.memset(tile, 0.0)
         for a in range(PASSES):
             nc.sync.dma_start(words[a][:], word_rows[a])
         for a in range(PASSES):
@@ -61,7 +60,7 @@ def tile_list_tabscat_silu_kernel(tc, tab, w, b, wgo, offs, offs2, out):
 
         windows = [hold.tile([P, T], F32, name=f"window{m}") for m in range(M_TILES)]
         nc.vector.memset(windows[0][:], 0.0)
-        nc.gpsimd.memset(windows[1][:], 0.0)
+        nc.vector.memset(windows[1][:], 0.0)
 
         warm = hold.tile([P, 1], F32, name="warm")
         nc.vector.memset(warm[:], 0.0)

@@ -60,7 +60,8 @@ def tile_list_tabscat_silu_kernel(tc, tab, w, b, wgo, offs, offs2, out):
 
         windows = [hold.tile([P, T], F32, name=f"window{m}") for m in range(M_TILES)]
         nc.vector.memset(windows[0][:], 0.0)
-        nc.vector.memset(windows[1][:], 0.0)
+        nc.vector.memset(windows[1][:, 0:8], 0.0)
+        nc.gpsimd.memset(windows[1][:], 0.0)
 
         warm = hold.tile([P, 1], F32, name="warm")
         nc.vector.memset(warm[:], 0.0)

import concourse.mybir as mybir

K, M, T, S = 1024, 256, 4096, 2048
P = 128
PASSES = K // 512
M_TILES = M // P
N_TILE = 512
SLICES = S // N_TILE
COLS = N_TILE // 16

F32 = mybir.dt.float32
BF16 = mybir.dt.bfloat16
I32 = mybir.dt.int32
U32 = mybir.dt.uint32
U16 = mybir.dt.uint16
U8 = mybir.dt.uint8
FP8X4 = mybir.dt.float8_e4m3fn_x4
MULT = mybir.AluOpType.mult
SILU = mybir.ActivationFunctionType.Silu

FLOPS = 2 * K * M * S


def tile_list_tabscat_silu_kernel(tc, tab, w, b, wgo, offs, offs2, out):
    nc = tc.nc
    with tc.tile_pool(name="hold", bufs=1) as hold, tc.psum_pool(name="psum", bufs=1) as psum:
        list_in = hold.tile([P, S // 16], U16, name="list_in")
        list_out = hold.tile([P, S // 16], U16, name="list_out")
        nc.sync.dma_start(list_in[:], offs)

        scales = hold.tile([P, T], U8, name="scales", align_bytes=64)
        scale_words = scales[:].bitcast(I32)
        nc.vector.memset(scale_words, 0)
        scale_rows = tab[:, 512 * T : 528 * T].rearrange("a (q t) -> a q t", q=16)
        for quad in range(4):
            rows = scale_rows[:, 4 * quad : 4 * quad + 4, :].bitcast(I32)
            if quad < 3:
                for a in range(PASSES):
                    p0 = 32 * quad + 4 * a
                    nc.sync.dma_start(scale_words[p0 : p0 + 4, :], rows[a])
            else:
                nc.sync.dma_start(scale_words[32 * quad : 32 * quad + 8, :], rows)

        words = [hold.tile([P, T], I32, name=f"words{a}", align_bytes=64) for a in range(PASSES)]
        w_raw = [hold.tile([P, 4, M], F32, name=f"w_raw{a}") for a in range(PASSES)]
        word_rows = [tab[a, 0 : 512 * T].rearrange("(p x) -> p x", p=P).bitcast(I32) for a in range(PASSES)]
        weight_out = hold.tile([P, S], F32, name="weight_out")
        for tile in (words[0][:, 0:8], words[1][:, 0:8]):
            nc.vector.memset(tile, 0)
        for tile in (w_raw[0][:, 0, 0:8], w_raw[1][:, 0, 0:8], weight_out[:, 0:8]):
            nc.vector.memset(tile, 0.0)
        for a in range(PASSES):
            nc.sync.dma_start(words[a][:], word_rows[a])
        for a in range(PASSES):
            nc.sync.dma_start(w_raw[a][:], w[512 * a : 512 * (a + 1), :].rearrange("(p j) n -> p j n", j=4))
        bias = hold.tile([P, M_TILES], F32, name="bias")
        nc.sync.dma_start(bias[:], b.rearrange("(m p) -> p m", p=P))
        nc.sync.dma_start(weight_out[:], wgo)
        nc.sync.dma_start(list_out[:], offs2)

        windows = [hold.tile([P, T], F32, name=f"window{m}") for m in range(M_TILES)]
        nc.vector.memset(windows[0][:], 0.0)
        nc.vector.memset(windows[1][:, 0:8], 0.0)
        nc.gpsimd.memset(windows[1][:], 0.0)

        warm = hold.tile([P, 1], F32, name="warm")
        nc.vector.memset(warm[:], 0.0)
        warmed = hold.tile([P, 1], F32, name="warmed")
        nc.scalar.activation(warmed[:], warm[:], SILU)

        picked_scales = hold.tile([P, S], U8, name="picked_scales", align_bytes=64)
        nc.vector.tensor_copy(picked_scales[:], scales[:].indirect(list_in[:]))
        picked_first = hold.tile([P, S], U32, name="picked_first", align_bytes=64)
        nc.vector.tensor_copy(picked_first[:], words[0][:].bitcast(U32).indirect(list_in[:]))

        w_inter = [
            hold.tile([P, PASSES, P, 4], BF16, name=f"w_inter{m}", tag=f"turn{m}", align_bytes=64) for m in range(M_TILES)
        ]
        w_codes = hold.tile([P, M_TILES, PASSES, P], U32, name="w_codes", align_bytes=64)
        w_scales = hold.tile([P, M_TILES, PASSES, P], U8, name="w_scales", align_bytes=64)
        for a in range(PASSES):
            for m in range(M_TILES):
                nc.scalar.copy(w_inter[m][:, a, :, :], w_raw[a][:, :, P * m : P * (m + 1)].rearrange("p j n -> p n j"))

        def quantise(m):
            nc.vector.quantize_mx(
                out=w_codes[:, m, :, :].rearrange("p a n -> p (a n)").bitcast(FP8X4),
                scales=w_scales[:, m, :, :].rearrange("p a n -> p (a n)"),
                in_=w_inter[m][:].rearrange("p a n j -> p (a n j)"),
            )

        def gather_half(h):
            half = hold.tile([P, S // 2], U32, name=f"picked_last{h}", tag="turn0" if h else "picked_last0", align_bytes=64)
            cols = slice(S // 32 * h, S // 32 * (h + 1))
            nc.vector.tensor_copy(half[:], words[1][:].bitcast(U32).indirect(list_in[:, cols]))
            return half


        results = [hold.tile([P, S], F32, name=f"result{m}") for m in range(M_TILES)]

        def multiply(m, s):
            cols = slice(N_TILE * s, N_TILE * (s + 1))
            inner = slice(N_TILE * (s % 2), N_TILE * (s % 2 + 1))
            rhs = [picked_first[:, cols], picked_last[s // 2][:, inner]]
            acc = psum.tile([P, N_TILE], F32, name=f"acc{m}_{s}")
            for a in range(PASSES):
                nc.tensor.matmul_mx(
                    out=acc[:],
                    lhsT=w_codes[:, m, a, :].bitcast(FP8X4),
                    lhsT_scale=w_scales[:, m, a, :],
                    rhs=rhs[a].bitcast(FP8X4),
                    rhs_scale=picked_scales[4 * a : P, cols],
                    start=(a == 0),
                    stop=(a == PASSES - 1),
                )
            nc.scalar.activation(results[m][:, cols], acc[:], SILU, bias=bias[:, m : m + 1])

        def scatter(m, first, last):
            cols = slice(N_TILE * first, N_TILE * last)
            nc.vector.tensor_tensor(
                windows[m][:].indirect(list_out[:, COLS * first : COLS * last]),
                results[m][:, cols],
                weight_out[:, cols],
                MULT,
            )

        picked_last = [gather_half(0)]
        quantise(0)
        picked_last.append(gather_half(1))
        quantise(1)
        for m in range(M_TILES):
            for s in range(SLICES):
                multiply(m, s)
        scatter(0, 0, 1)
        scatter(0, 1, SLICES)
        nc.sync.dma_start(out[0:P, :], windows[0][:])
        scatter(1, 0, SLICES)
        nc.sync.dma_start(out[P : 2 * P, :], windows[1][:])
